import numpy as np
import ml_dtypes


def mxq(x, axis, fmt="e4m3"):
    dtype, down = {"e4m3": (ml_dtypes.float8_e4m3fn, 7), "e5m2": (ml_dtypes.float8_e5m2, 14)}[fmt]
    v = np.moveaxis(np.asarray(x, np.float32).astype(ml_dtypes.bfloat16).astype(np.float64), axis, -1)
    blocks = v.reshape(v.shape[:-1] + (-1, 32))
    amax = np.abs(blocks).max(-1, keepdims=True)
    byte = np.maximum(np.where(amax > 0, np.frexp(amax)[1] - 1 + 127, 0) - down, 1)
    scale = np.exp2(byte - 127.0)
    codes = (blocks / scale).astype(np.float32).astype(dtype).astype(np.float64)
    return np.moveaxis((codes * scale).reshape(v.shape), -1, axis)


WIDE = False


def mx_kscale(k):
    if not WIDE:
        return np.ones(k)
    levels = np.array([10, -10, 5, -5, 0])
    if k % 512:
        return np.exp2(np.random.permutation(np.resize(levels, k // 32))).repeat(32)
    a = np.empty((k // 512, 16))
    for p in range(k // 512):
        a[p, :8] = np.random.permutation(np.resize(levels, 8))
        for g in range(8):
            far = levels[np.abs(levels - a[p, g]) >= 10]
            a[p, g + 8] = far[np.random.randint(len(far))]
    return np.exp2(a.ravel()).repeat(32)


def f64(x):
    return np.asarray(x).astype(np.float64)


def striped(idx):
    return np.tile(idx.reshape(-1, 16).T, (8, 1)).astype(np.uint16)


def unstriped(offs):
    return offs[:16].T.reshape(-1).astype(np.int64)


def pack_weight(w):
    k, n = w.shape
    w = f64(np.asarray(w, np.float32).astype(ml_dtypes.bfloat16)).reshape(k // 32, 32, n)
    amax = np.abs(w).max(1)
    byte = np.clip(np.where(amax > 0, np.frexp(amax)[1] - 1 + 127 - 7, 1), 1, 254)
    scaled = (w * np.exp2(127.0 - byte)[:, None, :]).reshape(k, n).astype(np.float32)
    words = np.ascontiguousarray(scaled.reshape(k // 512, 128, 4, n).transpose(0, 1, 3, 2)).astype(ml_dtypes.float8_e4m3fn).view(np.uint8)
    return words, np.ascontiguousarray(byte.astype(np.uint8).reshape(k // 512, 16, n))


def unpack_weight(words, scales):
    g, p, n, _ = words.shape
    vals = np.ascontiguousarray(words).view(ml_dtypes.float8_e4m3fn).astype(np.float64) * np.repeat(np.exp2(scales.astype(np.float64) - 127.0), 8, axis=1)[..., None]
    return vals.transpose(0, 1, 3, 2).reshape(g * 512, n)


def relu(v):
    return np.maximum(v, 0.0)


K, T, S, D, N = 1024, 4096, 1024, 8, 256
P = 2 ** 7


def setup_inputs():
    n = np.random.standard_normal
    s = mx_kscale(K)[:, None]
    packed_xT = pack_weight(n((K, T)) * s)
    return {
        "x_words": packed_xT[0],
        "x_scales": packed_xT[1],
        "w1": (n((K, N)) / np.sqrt(K) / s).astype(np.float32),
        "w2": (n((K, N)) / np.sqrt(K) / s).astype(np.float32),
        "dist2": (np.tile(np.random.uniform(0.0, 1.2, S), (P, 1))).astype(np.float32),
        "band": (-np.random.uniform(0.8, 1.9, (N, 1))).astype(np.float32),
        "offs": striped(np.random.permutation(T)[:S]),
    }


def reference(x_words, x_scales, w1, w2, dist2, band, offs):
    wt = (relu(f64(band) * f64(dist2)[:1] + 1.3)) ** 2
    xq = unpack_weight(x_words, x_scales)[:, unstriped(offs)]
    xv = mxq(f64(w1), 0, "e4m3").T @ xq
    sxj = wt * xv
    sx = sxj.reshape(len(sxj), -1, D).sum(axis=2)
    s0 = wt.reshape(len(wt), -1, D).sum(axis=2) + 0.2
    mx = sx / s0
    yv = mxq(f64(w2), 0, "e4m3").T @ xq
    syj = wt * yv
    sy = syj.reshape(len(syj), -1, D).sum(axis=2)
    my = sy / s0
    sxyj = (wt * (xv - np.repeat(mx, D, axis=1))) * (yv - np.repeat(my, D, axis=1))
    sxy = sxyj.reshape(len(sxyj), -1, D).sum(axis=2)
    sxxj = wt * ((xv - np.repeat(mx, D, axis=1)) ** 2)
    sxx = sxxj.reshape(len(sxxj), -1, D).sum(axis=2)
    slope = sxy / (sxx + 0.3)
    return slope + 0.2 * (my - (slope * mx))

@@ -1,0 +1,236 @@
+from contextlib import ExitStack
+
+import concourse.mybir as mybir
+from concourse.masks import make_identity
+
+F32 = mybir.dt.float32
+BF16 = mybir.dt.bfloat16
+I32 = mybir.dt.int32
+U32 = mybir.dt.uint32
+U16 = mybir.dt.uint16
+U8 = mybir.dt.uint8
+FP8X4 = mybir.dt.float8_e4m3fn_x4
+ALU = mybir.AluOpType
+ACT = mybir.ActivationFunctionType
+
+K, T, S, D, N = 1024, 4096, 1024, 8, 256
+P = 128
+PASSES = 2
+BLOCKS = 2
+HALVES = 2
+HALF = 512
+V = 128
+VH = 64
+FLOPS = 2 * 2 * K * N * S
+
+
+def tile_picked_ygwrg_coef_p_kernel(tc, x_words, x_scales, w1, w2, dist2, band, offs, out):
+    nc = tc.nc
+    with ExitStack() as ctx:
+        keep = ctx.enter_context(tc.tile_pool(name="keep", bufs=1))
+        psum = ctx.enter_context(tc.psum_pool(name="psum", bufs=1))
+
+        def bank(index, shape):
+            return psum.tile(shape, F32, name="bank%d" % index, tag="bank%d" % index)
+
+        scale_window = keep.tile([P, T], U8, name="scale_window", tag="shared0", align_bytes=64)
+        nc.sync.dma_start(
+            scale_window[0:32, :].bitcast(I32), x_scales.rearrange("g q c -> (g q) c").bitcast(I32)
+        )
+        offsets = keep.tile([P, S // 16], U16, name="offsets")
+        nc.sync.dma_start(offsets[:], offs)
+        nc.gpsimd.memset(scale_window[32:64, :].bitcast(I32), 0)
+        nc.vector.memset(scale_window[64:P, :].bitcast(I32), 0)
+        dist_vd = keep.tile([P, D], F32, name="dist_vd", tag="shared1", align_bytes=64)
+        nc.scalar.dma_start(dist_vd[:], dist2[0].rearrange("(v d) -> v d", d=D))
+        band_pb = keep.tile([P, BLOCKS], F32, name="band_pb", tag="shared3", align_bytes=64)
+        with nc.allow_non_contiguous_dma(reason="one value a partition"):
+            nc.scalar.dma_start(band_pb[:], band.rearrange("(b p) o -> p (b o)", p=P))
+
+        def load_words(g, tag):
+            t = keep.tile([P, T], I32, name="word_window%d" % g, tag=tag, align_bytes=64)
+            nc.sync.dma_start(t[:], x_words[g].rearrange("p c r -> p (c r)").bitcast(I32))
+            return t
+
+        def load_weights(mat, g, tag):
+            w = (w1, w2)[mat]
+            t = keep.tile([P, 4, N], F32, name="raw%d%d" % (mat, g), tag=tag, align_bytes=64)
+            nc.sync.dma_start(t[:], w[512 * g : 512 * (g + 1), :].rearrange("(p j) m -> p j m", j=4))
+            raw[mat, g] = t
+
+        raw = {}
+        word_window = [load_words(0, "word_window0")]
+
+        ident = keep.tile([P, P], F32, name="ident")
+        make_identity(nc, ident[:])
+        one = keep.tile([P, 1], F32, name="one")
+        nc.gpsimd.memset(one[:], 1.0)
+        table_preload = keep.tile([P, 1], F32, name="table_preload")
+        nc.scalar.activation(table_preload[:], one[:], ACT.Abs_reciprocal_sqrt)
+
+        picked_rows = keep.tile([P, S], U8, name="picked_rows", align_bytes=64)
+        nc.vector.tensor_copy(picked_rows[:], scale_window[:].indirect(offsets[:]))
+        x_planes = []
+        for g in range(PASSES):
+            t = keep.tile([P, S], U8, name="x_planes%d" % g, align_bytes=64)
+            nc.gpsimd.memset(t[:].bitcast(I32), 0)
+            x_planes.append(t)
+        for g in range(PASSES):
+            for q in range(4):
+                first = 16 * g + 4 * q
+                (nc.scalar, nc.gpsimd)[g].dma_start(
+                    x_planes[g][32 * q : 32 * q + 4, :].bitcast(I32),
+                    picked_rows[first : first + 4, :].bitcast(I32),
+                )
+
+        dist_banks = []
+        for dh in range(2):
+            t = bank(4 + dh, [P, 4, V])
+            for dl in range(4):
+                d = 4 * dh + dl
+                nc.tensor.transpose(t[:, dl, :], dist_vd[:, d : d + 1].to_broadcast([P, P]), ident[:])
+            dist_banks.append(t)
+        word_window.append(load_words(1, "shared0"))
+        load_weights(0, 0, "shared1")
+        wt = []
+        s0_bank = bank(6, [P, BLOCKS, P])
+
+        def group_sum(dst, src):
+            for d in range(D):
+                nc.tensor.matmul(dst, src[:, d, :], ident[:], start=(d == 0), stop=(d == D - 1), is_transpose=True)
+
+        for b in range(BLOCKS):
+            root = keep.tile([P, D, V], F32, name="root%d" % b, tag=("shared2", "shared4")[b], align_bytes=64)
+            t = keep.tile([P, D, V], F32, name="wt%d" % b)
+            for dh in range(2):
+                nc.scalar.activation(
+                    root[:, 4 * dh : 4 * dh + 4, :], dist_banks[dh][:], ACT.Relu, bias=1.3, scale=band_pb[:, b : b + 1]
+                )
+            nc.scalar.activation(t[:], root[:], ACT.Square)
+            group_sum(s0_bank[:, b, :], t)
+            wt.append(t)
+        load_weights(0, 1, "shared2")
+        load_weights(1, 0, "shared3")
+        load_weights(1, 1, "shared4")
+        s0 = keep.tile([P, BLOCKS, P], F32, name="s0")
+        rs = keep.tile([P, BLOCKS, P], F32, name="rs")
+        gn = keep.tile([P, BLOCKS, P], F32, name="gn")
+        kn = keep.tile([P, BLOCKS, P], F32, name="kn")
+        nc.scalar.activation(s0[:], s0_bank[:], ACT.Identity, bias=0.2)
+        nc.vector.reciprocal(rs[:], s0[:])
+        nc.scalar.activation(gn[:], rs[:], ACT.Copy, scale=-0.2)
+        nc.vector.scalar_tensor_tensor(kn[:], gn[:], 1.0, rs[:], ALU.subtract, ALU.mult)
+
+        words = {}
+        for g in range(PASSES):
+            for h in range(HALVES):
+                t = keep.tile([P, HALF], U32, name="words%d%d" % (g, h), align_bytes=64)
+                nc.vector.tensor_copy(
+                    t[:], word_window[g][:].bitcast(U32).indirect(offsets[:, 32 * h : 32 * (h + 1)])
+                )
+                words[g, h] = t
+
+        codes, planes = {}, {}
+
+        def quantise(mat, g):
+            grouped = keep.tile([P, N, 4], BF16, name="grouped%d%d" % (mat, g), align_bytes=64)
+            (nc.vector.tensor_copy if (mat, g) == (0, 1) else nc.scalar.copy)(
+                grouped[:].rearrange("p (c i) j -> p c j i", i=4),
+                raw[mat, g][:].rearrange("p j (c i) -> p c j i", i=4),
+            )
+            c = keep.tile([P, N], U32, name="codes%d%d" % (mat, g), align_bytes=64)
+            s = keep.tile([P, N], U8, name="planes%d%d" % (mat, g), align_bytes=64)
+            nc.vector.quantize_mx(c[:].bitcast(FP8X4), s[:], grouped[:].rearrange("p m j -> p (m j)"))
+            codes[mat, g], planes[mat, g] = c, s
+
+        def product(mat, b, h, index):
+            t = bank(index, [P, HALF])
+            cols = slice(P * b, P * (b + 1))
+            for g in range(PASSES):
+                nc.tensor.matmul_mx(
+                    t[:],
+                    lhsT=codes[mat, g][:, cols].bitcast(FP8X4),
+                    lhsT_scale=planes[mat, g][:, cols],
+                    rhs=words[g, h][:].bitcast(FP8X4),
+                    rhs_scale=x_planes[g][:, HALF * h : HALF * (h + 1)],
+                    start=(g == 0),
+                    stop=(g == PASSES - 1),
+                )
+            return t[:].rearrange("p (v d) -> p d v", d=D)
+
+        def half(t, h):
+            return t[:, :, VH * h : VH * (h + 1)]
+
+        def wide(name):
+            return keep.tile([P, D, V], F32, name=name)
+
+        def small(name):
+            return keep.tile([P, BLOCKS, P], F32, name=name)
+
+        for g in range(PASSES):
+            quantise(0, g)
+        sx = bank(6, [P, BLOCKS, P])
+        sxx = bank(7, [P, BLOCKS, P])
+        wx = [wide("wx0"), wide("wx1")]
+        wxx = [wide("wxx0"), wide("wxx1")]
+        wy = [wide("wy0"), wide("wy1")]
+        wxy = [wide("wxy0"), wide("wxy1")]
+        xsq, ys = wide("xsq"), wide("ys")
+        xv = [[product(0, b, h, 2 * b + h) for h in range(HALVES)] for b in range(BLOCKS)]
+        for h in range(HALVES):
+            nc.vector.tensor_tensor(half(wx[0], h), xv[0][h], half(wt[0], h), ALU.mult)
+            nc.scalar.activation(half(xsq, h), xv[0][h], ACT.Square)
+        group_sum(sx[:, 0, :], wx[0])
+        for dh in range(2):
+            ds = slice(4 * dh, 4 * dh + 4)
+            nc.gpsimd.tensor_tensor(wxx[0][:, ds, :], xsq[:, ds, :], wt[0][:, ds, :], ALU.mult)
+        for h in range(HALVES):
+            nc.vector.tensor_tensor(half(wx[1], h), xv[1][h], half(wt[1], h), ALU.mult)
+        group_sum(sx[:, 1, :], wx[1])
+        for g in range(PASSES):
+            quantise(1, g)
+        yv = [[product(1, 0, h, 4 + h) for h in range(HALVES)]]
+        for h in range(HALVES):
+            nc.vector.tensor_tensor(half(wxx[1], h), xv[1][h], half(wx[1], h), ALU.mult)
+        yv.append([product(1, 1, h, h) for h in range(HALVES)])
+        for h in range(HALVES):
+            nc.scalar.copy(half(ys, h), yv[1][h])
+            nc.gpsimd.tensor_tensor(half(wy[1], h), half(ys, h), half(wt[1], h), ALU.mult)
+
+        km, dd, gs, den, ars, rec, gg, hk, hh, t1, t2 = [
+            small(n) for n in ("km", "dd", "gs", "den", "ars", "rec", "gg", "hk", "hh", "t1", "t2")
+        ]
+        nc.vector.tensor_tensor(km[:], sx[:], kn[:], ALU.mult)
+        nc.vector.tensor_tensor(gs[:], sx[:], gn[:], ALU.mult)
+        nc.vector.tensor_tensor(dd[:], sx[:], km[:], ALU.mult)
+        group_sum(sxx[:, 1, :], wxx[1])
+        group_sum(sxx[:, 0, :], wxx[0])
+        nc.vector.tensor_tensor(den[:], sxx[:], dd[:], ALU.add)
+        nc.scalar.activation(ars[:], den[:], ACT.Abs_reciprocal_sqrt, bias=0.3)
+        nc.scalar.activation(rec[:], ars[:], ACT.Square)
+        nc.vector.scalar_tensor_tensor(gg[:], gs[:], 1.0, rec[:], ALU.add, ALU.mult)
+        nc.gpsimd.tensor_tensor(hk[:], gg[:], km[:], ALU.mult)
+        nc.gpsimd.tensor_tensor(hh[:], hk[:], gn[:], ALU.subtract)
+
+        sy = bank(2, [P, BLOCKS, P])
+        for h in range(HALVES):
+            nc.vector.tensor_tensor(half(wy[0], h), yv[0][h], half(wt[0], h), ALU.mult)
+        group_sum(sy[:, 0, :], wy[0])
+        for h in range(HALVES):
+            nc.vector.tensor_tensor(half(wxy[0], h), yv[0][h], half(wx[0], h), ALU.mult)
+        sxy = [bank(3, [P, P])]
+        group_sum(sxy[0][:], wxy[0])
+        for h in range(HALVES):
+            nc.vector.tensor_tensor(half(wxy[1], h), yv[1][h], half(wx[1], h), ALU.mult)
+        group_sum(sy[:, 1, :], wy[1])
+        sxy.append(bank(4, [P, P]))
+        group_sum(sxy[1][:], wxy[1])
+        nc.vector.tensor_tensor(t2[:], sy[:], hh[:], ALU.mult)
+        for b in range(BLOCKS):
+            nc.vector.tensor_tensor(t1[:, b], sxy[b][:], gg[:, b], ALU.mult)
+            turned = bank(6 + b, [P, V])
+            nc.tensor.matmul(turned[:], t2[:, b], ident[:], start=True, stop=False, is_transpose=True)
+            nc.tensor.matmul(turned[:], t1[:, b], ident[:], start=False, stop=True, is_transpose=True)
+            result = keep.tile([P, V], F32, name="result%d" % b)
+            nc.scalar.copy(result[:], turned[:])
+            nc.sync.dma_start(out[P * b : P * (b + 1), :], result[:])

@@ -41,9 +41,9 @@ def tile_picked_ygwrg_coef_p_kernel(tc, x_words, x_scales, w1, w2, dist2, band, 
         nc.sync.dma_start(offsets[:], offs)
         nc.gpsimd.memset(scale_window[32:64, :].bitcast(I32), 0)
         nc.vector.memset(scale_window[64:P, :].bitcast(I32), 0)
-        dist_vd = keep.tile([P, D], F32, name="dist_vd", tag="shared1", align_bytes=64)
+        dist_vd = keep.tile([P, D], F32, name="dist_vd")
         nc.scalar.dma_start(dist_vd[:], dist2[0].rearrange("(v d) -> v d", d=D))
-        band_pb = keep.tile([P, BLOCKS], F32, name="band_pb", tag="shared3", align_bytes=64)
+        band_pb = keep.tile([P, BLOCKS], F32, name="band_pb")
         with nc.allow_non_contiguous_dma(reason="one value a partition"):
             nc.scalar.dma_start(band_pb[:], band.rearrange("(b p) o -> p (b o)", p=P))
 
@@ -60,6 +60,8 @@ def tile_picked_ygwrg_coef_p_kernel(tc, x_words, x_scales, w1, w2, dist2, band, 
 
         raw = {}
         word_window = [load_words(0, "word_window0")]
+        load_weights(0, 0, "raw00")
+        word_window.append(load_words(1, "word_window1"))
 
         ident = keep.tile([P, P], F32, name="ident")
         make_identity(nc, ident[:])
@@ -78,7 +80,7 @@ def tile_picked_ygwrg_coef_p_kernel(tc, x_words, x_scales, w1, w2, dist2, band, 
         for g in range(PASSES):
             for q in range(4):
                 first = 16 * g + 4 * q
-                (nc.scalar, nc.gpsimd)[g].dma_start(
+                (nc.sync, nc.gpsimd)[g].dma_start(
                     x_planes[g][32 * q : 32 * q + 4, :].bitcast(I32),
                     picked_rows[first : first + 4, :].bitcast(I32),
                 )
@@ -90,36 +92,46 @@ def tile_picked_ygwrg_coef_p_kernel(tc, x_words, x_scales, w1, w2, dist2, band, 
                 d = 4 * dh + dl
                 nc.tensor.transpose(t[:, dl, :], dist_vd[:, d : d + 1].to_broadcast([P, P]), ident[:])
             dist_banks.append(t)
-        word_window.append(load_words(1, "shared0"))
-        load_weights(0, 0, "shared1")
         wt = []
-        s0_bank = bank(6, [P, BLOCKS, P])
 
-        def group_sum(dst, src):
-            for d in range(D):
-                nc.tensor.matmul(dst, src[:, d, :], ident[:], start=(d == 0), stop=(d == D - 1), is_transpose=True)
+        def group_sum(dst, src, extra=()):
+            terms = [src[:, d, :] for d in range(D)] + list(extra)
+            for i, term in enumerate(terms):
+                nc.tensor.matmul(dst, term, ident[:], start=(i == 0), stop=(i == len(terms) - 1), is_transpose=True)
 
+        k1n = keep.tile([P, BLOCKS, P], F32, name="k1n")
+        ridge = keep.tile([P, BLOCKS, V], F32, name="ridge")
         for b in range(BLOCKS):
-            root = keep.tile([P, D, V], F32, name="root%d" % b, tag=("shared2", "shared4")[b], align_bytes=64)
-            t = keep.tile([P, D, V], F32, name="wt%d" % b)
+            root = keep.tile([P, D, V], F32, name="root%d" % b, tag="root%d" % b, align_bytes=64)
+            square = keep.tile([P, D, V], F32, name="square%d" % b, tag="square%d" % b, align_bytes=64)
             for dh in range(2):
                 nc.scalar.activation(
                     root[:, 4 * dh : 4 * dh + 4, :], dist_banks[dh][:], ACT.Relu, bias=1.3, scale=band_pb[:, b : b + 1]
                 )
-            nc.scalar.activation(t[:], root[:], ACT.Square)
-            group_sum(s0_bank[:, b, :], t)
+            for dh in range(2):
+                ds = slice(4 * dh, 4 * dh + 4)
+                if b == 0:
+                    nc.vector.tensor_tensor(square[:, ds, :], root[:, ds, :], root[:, ds, :], ALU.mult)
+                else:
+                    nc.scalar.activation(square[:, ds, :], root[:, ds, :], ACT.Square)
+            s0_bank = bank((2, 6)[b], [P, P])
+            group_sum(s0_bank[:], square)
+            q = keep.tile([P, P], F32, name="q%d" % b)
+            rs = keep.tile([P, P], F32, name="rs%d" % b)
+            nc.scalar.activation(q[:], s0_bank[:], ACT.Abs_reciprocal_sqrt, bias=0.2)
+            nc.scalar.activation(rs[:], q[:], ACT.Square)
+            rs_bank = bank((3, 7)[b], [P, V])
+            nc.tensor.transpose(rs_bank[:], rs[:], ident[:])
+            t = keep.tile([P, D, V], F32, name="wt%d" % b)
+            nc.vector.tensor_tensor(
+                t[:], square[:], rs_bank[:].unsqueeze(1).to_broadcast([P, D, V]), ALU.mult
+            )
+            nc.scalar.activation(k1n[:, b, :], rs[:], ACT.Identity, scale=-0.2, bias=-1.0)
+            nc.scalar.activation(ridge[:, b, :], rs_bank[:], ACT.Copy, scale=0.3)
             wt.append(t)
-        load_weights(0, 1, "shared2")
-        load_weights(1, 0, "shared3")
-        load_weights(1, 1, "shared4")
-        s0 = keep.tile([P, BLOCKS, P], F32, name="s0")
-        rs = keep.tile([P, BLOCKS, P], F32, name="rs")
-        gn = keep.tile([P, BLOCKS, P], F32, name="gn")
-        kn = keep.tile([P, BLOCKS, P], F32, name="kn")
-        nc.scalar.activation(s0[:], s0_bank[:], ACT.Identity, bias=0.2)
-        nc.vector.reciprocal(rs[:], s0[:])
-        nc.scalar.activation(gn[:], rs[:], ACT.Copy, scale=-0.2)
-        nc.vector.scalar_tensor_tensor(kn[:], gn[:], 1.0, rs[:], ALU.subtract, ALU.mult)
+        load_weights(0, 1, "shared0")
+        load_weights(1, 0, "root1")
+        load_weights(1, 1, "square0")
 
         words = {}
         for g in range(PASSES):
@@ -132,25 +144,27 @@ def tile_picked_ygwrg_coef_p_kernel(tc, x_words, x_scales, w1, w2, dist2, band, 
 
         codes, planes = {}, {}
 
-        def quantise(mat, g):
-            grouped = keep.tile([P, N, 4], BF16, name="grouped%d%d" % (mat, g), align_bytes=64)
-            (nc.vector.tensor_copy if (mat, g) == (0, 1) else nc.scalar.copy)(
+        def quantise(mat, g, first, width, cast):
+            name = "%d%d%d" % (mat, g, first)
+            grouped = keep.tile([P, width, 4], BF16, name="grouped" + name, tag="grouped" + name, align_bytes=64)
+            cast(
                 grouped[:].rearrange("p (c i) j -> p c j i", i=4),
-                raw[mat, g][:].rearrange("p j (c i) -> p c j i", i=4),
+                raw[mat, g][:, :, first : first + width].rearrange("p j (c i) -> p c j i", i=4),
             )
-            c = keep.tile([P, N], U32, name="codes%d%d" % (mat, g), align_bytes=64)
-            s = keep.tile([P, N], U8, name="planes%d%d" % (mat, g), align_bytes=64)
+            c = keep.tile([P, width], U32, name="codes" + name, align_bytes=64)
+            s = keep.tile([P, width], U8, name="planes" + name, align_bytes=64)
             nc.vector.quantize_mx(c[:].bitcast(FP8X4), s[:], grouped[:].rearrange("p m j -> p (m j)"))
-            codes[mat, g], planes[mat, g] = c, s
+            for m0 in range(0, width, P):
+                codes[mat, g, (first + m0) // P] = c[:, m0 : m0 + P]
+                planes[mat, g, (first + m0) // P] = s[:, m0 : m0 + P]
 
         def product(mat, b, h, index):
             t = bank(index, [P, HALF])
-            cols = slice(P * b, P * (b + 1))
             for g in range(PASSES):
                 nc.tensor.matmul_mx(
                     t[:],
-                    lhsT=codes[mat, g][:, cols].bitcast(FP8X4),
-                    lhsT_scale=planes[mat, g][:, cols],
+                    lhsT=codes[mat, g, b].bitcast(FP8X4),
+                    lhsT_scale=planes[mat, g, b],
                     rhs=words[g, h][:].bitcast(FP8X4),
                     rhs_scale=x_planes[g][:, HALF * h : HALF * (h + 1)],
                     start=(g == 0),
@@ -161,74 +175,86 @@ def tile_picked_ygwrg_coef_p_kernel(tc, x_words, x_scales, w1, w2, dist2, band, 
         def half(t, h):
             return t[:, :, VH * h : VH * (h + 1)]
 
+
         def wide(name):
             return keep.tile([P, D, V], F32, name=name)
 
         def small(name):
             return keep.tile([P, BLOCKS, P], F32, name=name)
 
-        for g in range(PASSES):
-            quantise(0, g)
-        sx = bank(6, [P, BLOCKS, P])
+        def warm_up(index):
+            t = bank(index, [P, HALF])
+            for g in range(PASSES):
+                nc.tensor.matmul_mx(
+                    t[:],
+                    lhsT=words[1, 0][:, 0:P].bitcast(FP8X4),
+                    lhsT_scale=x_planes[1][:, 0:P],
+                    rhs=words[g, 0][:].bitcast(FP8X4),
+                    rhs_scale=x_planes[g][:, 0:HALF],
+                    start=(g == 0),
+                    stop=(g == PASSES - 1),
+                )
+
+        quantise(0, 0, 0, N, nc.scalar.copy)
+        quantise(0, 1, 0, P, nc.scalar.copy)
+        quantise(0, 1, P, P, nc.scalar.copy)
+        mx = bank(6, [P, BLOCKS, P])
         sxx = bank(7, [P, BLOCKS, P])
         wx = [wide("wx0"), wide("wx1")]
         wxx = [wide("wxx0"), wide("wxx1")]
         wy = [wide("wy0"), wide("wy1")]
         wxy = [wide("wxy0"), wide("wxy1")]
         xsq, ys = wide("xsq"), wide("ys")
+        km, dd, nn, den, ars, rec, gg, hk, t1, t2 = [
+            small(n) for n in ("km", "dd", "nn", "den", "ars", "rec", "gg", "hk", "t1", "t2")
+        ]
         xv = [[product(0, b, h, 2 * b + h) for h in range(HALVES)] for b in range(BLOCKS)]
-        for h in range(HALVES):
-            nc.vector.tensor_tensor(half(wx[0], h), xv[0][h], half(wt[0], h), ALU.mult)
-            nc.scalar.activation(half(xsq, h), xv[0][h], ACT.Square)
-        group_sum(sx[:, 0, :], wx[0])
-        for dh in range(2):
-            ds = slice(4 * dh, 4 * dh + 4)
-            nc.gpsimd.tensor_tensor(wxx[0][:, ds, :], xsq[:, ds, :], wt[0][:, ds, :], ALU.mult)
-        for h in range(HALVES):
-            nc.vector.tensor_tensor(half(wx[1], h), xv[1][h], half(wt[1], h), ALU.mult)
-        group_sum(sx[:, 1, :], wx[1])
         for g in range(PASSES):
-            quantise(1, g)
-        yv = [[product(1, 0, h, 4 + h) for h in range(HALVES)]]
+            quantise(1, g, 0, N, nc.scalar.copy)
+        yv1 = [product(1, 1, h, 4 + h) for h in range(HALVES)]
+        for b in range(BLOCKS):
+            for h in range(HALVES):
+                nc.vector.tensor_tensor(half(wx[b], h), xv[b][h], half(wt[b], h), ALU.mult)
+            group_sum(mx[:, b, :], wx[b])
+        for h in range(HALVES):
+            nc.scalar.activation(half(xsq, h), xv[0][h], ACT.Square)
+            nc.gpsimd.tensor_tensor(half(wxx[0], h), half(xsq, h), half(wt[0], h), ALU.mult)
         for h in range(HALVES):
             nc.vector.tensor_tensor(half(wxx[1], h), xv[1][h], half(wx[1], h), ALU.mult)
-        yv.append([product(1, 1, h, h) for h in range(HALVES)])
-        for h in range(HALVES):
-            nc.scalar.copy(half(ys, h), yv[1][h])
+        for h in range(1):
+            nc.scalar.copy(half(ys, h), yv1[h])
             nc.gpsimd.tensor_tensor(half(wy[1], h), half(ys, h), half(wt[1], h), ALU.mult)
-
-        km, dd, gs, den, ars, rec, gg, hk, hh, t1, t2 = [
-            small(n) for n in ("km", "dd", "gs", "den", "ars", "rec", "gg", "hk", "hh", "t1", "t2")
-        ]
-        nc.vector.tensor_tensor(km[:], sx[:], kn[:], ALU.mult)
-        nc.vector.tensor_tensor(gs[:], sx[:], gn[:], ALU.mult)
-        nc.vector.tensor_tensor(dd[:], sx[:], km[:], ALU.mult)
-        group_sum(sxx[:, 1, :], wxx[1])
-        group_sum(sxx[:, 0, :], wxx[0])
+        nc.vector.tensor_tensor(km[:], mx[:], k1n[:], ALU.mult)
+        nc.vector.tensor_tensor(dd[:], mx[:], km[:], ALU.mult)
+        nc.scalar.activation(nn[:], mx[:], ACT.Identity, bias=1.0, scale=-0.2)
+        for h in range(HALVES):
+            if h >= 1:
+                nc.vector.tensor_tensor(half(wy[1], h), yv1[h], half(wt[1], h), ALU.mult)
+            nc.vector.tensor_tensor(half(wxy[1], h), yv1[h], half(wx[1], h), ALU.mult)
+        yv0 = [product(1, 0, h, (4, 5)[h]) for h in range(HALVES)]
+        for b in (1, 0):
+            group_sum(sxx[:, b, :], wxx[b], [ridge[:, b, :]])
         nc.vector.tensor_tensor(den[:], sxx[:], dd[:], ALU.add)
-        nc.scalar.activation(ars[:], den[:], ACT.Abs_reciprocal_sqrt, bias=0.3)
+        nc.scalar.activation(ars[:], den[:], ACT.Abs_reciprocal_sqrt)
         nc.scalar.activation(rec[:], ars[:], ACT.Square)
-        nc.vector.scalar_tensor_tensor(gg[:], gs[:], 1.0, rec[:], ALU.add, ALU.mult)
-        nc.gpsimd.tensor_tensor(hk[:], gg[:], km[:], ALU.mult)
-        nc.gpsimd.tensor_tensor(hh[:], hk[:], gn[:], ALU.subtract)
-
-        sy = bank(2, [P, BLOCKS, P])
-        for h in range(HALVES):
-            nc.vector.tensor_tensor(half(wy[0], h), yv[0][h], half(wt[0], h), ALU.mult)
-        group_sum(sy[:, 0, :], wy[0])
-        for h in range(HALVES):
-            nc.vector.tensor_tensor(half(wxy[0], h), yv[0][h], half(wx[0], h), ALU.mult)
-        sxy = [bank(3, [P, P])]
-        group_sum(sxy[0][:], wxy[0])
-        for h in range(HALVES):
-            nc.vector.tensor_tensor(half(wxy[1], h), yv[1][h], half(wx[1], h), ALU.mult)
-        group_sum(sy[:, 1, :], wy[1])
-        sxy.append(bank(4, [P, P]))
+        nc.vector.tensor_tensor(gg[:], nn[:], rec[:], ALU.mult)
+        nc.vector.tensor_tensor(hk[:], gg[:], km[:], ALU.mult)
+        my = bank(0, [P, BLOCKS, P])
+        sxy = [bank(2, [P, P]), bank(1, [P, P])]
         group_sum(sxy[1][:], wxy[1])
-        nc.vector.tensor_tensor(t2[:], sy[:], hh[:], ALU.mult)
-        for b in range(BLOCKS):
+        group_sum(my[:, 1, :], wy[1])
+        for h in range(HALVES):
+            nc.vector.tensor_tensor(half(wy[0], h), yv0[h], half(wt[0], h), ALU.mult)
+        group_sum(my[:, 0, :], wy[0])
+        nc.vector.tensor_tensor(half(wxy[0], 0), yv0[0], half(wx[0], 0), ALU.mult)
+        for dh in range(2):
+            ds = slice(4 * dh, 4 * dh + 4)
+            nc.vector.tensor_tensor(half(wxy[0], 1)[:, ds, :], yv0[1][:, ds, :], half(wx[0], 1)[:, ds, :], ALU.mult)
+        group_sum(sxy[0][:], wxy[0])
+        for b in (1, 0):
+            nc.vector.scalar_tensor_tensor(t2[:, b], hk[:, b], 0.2, my[:, b], ALU.add, ALU.mult)
             nc.vector.tensor_tensor(t1[:, b], sxy[b][:], gg[:, b], ALU.mult)
-            turned = bank(6 + b, [P, V])
+            turned = bank((6, 7)[b], [P, V])
             nc.tensor.matmul(turned[:], t2[:, b], ident[:], start=True, stop=False, is_transpose=True)
             nc.tensor.matmul(turned[:], t1[:, b], ident[:], start=False, stop=True, is_transpose=True)
             result = keep.tile([P, V], F32, name="result%d" % b)

@@ -37,12 +37,12 @@ def tile_picked_ygwrg_coef_p_kernel(tc, x_words, x_scales, w1, w2, dist2, band, 
         nc.sync.dma_start(
             scale_window[0:32, :].bitcast(I32), x_scales.rearrange("g q c -> (g q) c").bitcast(I32)
         )
+        dist_vd = keep.tile([P, D], F32, name="dist_vd")
+        nc.sync.dma_start(dist_vd[:], dist2[0].rearrange("(v d) -> v d", d=D))
         offsets = keep.tile([P, S // 16], U16, name="offsets")
         nc.sync.dma_start(offsets[:], offs)
         nc.gpsimd.memset(scale_window[32:64, :].bitcast(I32), 0)
         nc.vector.memset(scale_window[64:P, :].bitcast(I32), 0)
-        dist_vd = keep.tile([P, D], F32, name="dist_vd")
-        nc.scalar.dma_start(dist_vd[:], dist2[0].rearrange("(v d) -> v d", d=D))
         band_pb = keep.tile([P, BLOCKS], F32, name="band_pb")
         with nc.allow_non_contiguous_dma(reason="one value a partition"):
             nc.scalar.dma_start(band_pb[:], band.rearrange("(b p) o -> p (b o)", p=P))
@@ -116,8 +116,8 @@ def tile_picked_ygwrg_coef_p_kernel(tc, x_words, x_scales, w1, w2, dist2, band, 
                     nc.scalar.activation(square[:, ds, :], root[:, ds, :], ACT.Square)
             s0_bank = bank((2, 6)[b], [P, P])
             group_sum(s0_bank[:], square)
-            q = keep.tile([P, P], F32, name="q%d" % b)
-            rs = keep.tile([P, P], F32, name="rs%d" % b)
+            q = keep.tile([P, P], F32, name="q%d" % b, tag="q%d" % b, align_bytes=64)
+            rs = keep.tile([P, P], F32, name="rs%d" % b, tag="rs%d" % b, align_bytes=64)
             nc.scalar.activation(q[:], s0_bank[:], ACT.Abs_reciprocal_sqrt, bias=0.2)
             nc.scalar.activation(rs[:], q[:], ACT.Square)
             rs_bank = bank((3, 7)[b], [P, V])
@@ -131,27 +131,26 @@ def tile_picked_ygwrg_coef_p_kernel(tc, x_words, x_scales, w1, w2, dist2, band, 
             wt.append(t)
         load_weights(0, 1, "shared0")
         load_weights(1, 0, "root1")
-        load_weights(1, 1, "square0")
+        load_weights(1, 1, "q0")
 
         words = {}
-        for g in range(PASSES):
+
+        def gather_words(g, tag):
+            t = keep.tile([P, S], U32, name="words%d" % g, tag=tag, align_bytes=64)
+            nc.vector.tensor_copy(t[:], word_window[g][:].bitcast(U32).indirect(offsets[:]))
             for h in range(HALVES):
-                t = keep.tile([P, HALF], U32, name="words%d%d" % (g, h), align_bytes=64)
-                nc.vector.tensor_copy(
-                    t[:], word_window[g][:].bitcast(U32).indirect(offsets[:, 32 * h : 32 * (h + 1)])
-                )
-                words[g, h] = t
+                words[g, h] = t[:, HALF * h : HALF * (h + 1)]
 
         codes, planes = {}, {}
 
-        def quantise(mat, g, first, width, cast):
+        def quantise(mat, g, first, width, cast, tag=None, code_tag=None):
             name = "%d%d%d" % (mat, g, first)
-            grouped = keep.tile([P, width, 4], BF16, name="grouped" + name, tag="grouped" + name, align_bytes=64)
+            grouped = keep.tile([P, width, 4], BF16, name="grouped" + name, tag=tag or "grouped" + name, align_bytes=64)
             cast(
                 grouped[:].rearrange("p (c i) j -> p c j i", i=4),
                 raw[mat, g][:, :, first : first + width].rearrange("p j (c i) -> p c j i", i=4),
             )
-            c = keep.tile([P, width], U32, name="codes" + name, align_bytes=64)
+            c = keep.tile([P, width], U32, name="codes" + name, tag=code_tag or "codes" + name, align_bytes=64)
             s = keep.tile([P, width], U8, name="planes" + name, align_bytes=64)
             nc.vector.quantize_mx(c[:].bitcast(FP8X4), s[:], grouped[:].rearrange("p m j -> p (m j)"))
             for m0 in range(0, width, P):
@@ -165,7 +164,7 @@ def tile_picked_ygwrg_coef_p_kernel(tc, x_words, x_scales, w1, w2, dist2, band, 
                     t[:],
                     lhsT=codes[mat, g, b].bitcast(FP8X4),
                     lhsT_scale=planes[mat, g, b],
-                    rhs=words[g, h][:].bitcast(FP8X4),
+                    rhs=words[g, h].bitcast(FP8X4),
                     rhs_scale=x_planes[g][:, HALF * h : HALF * (h + 1)],
                     start=(g == 0),
                     stop=(g == PASSES - 1),
@@ -195,13 +194,13 @@ def tile_picked_ygwrg_coef_p_kernel(tc, x_words, x_scales, w1, w2, dist2, band, 
                     stop=(g == PASSES - 1),
                 )
 
-        quantise(0, 0, 0, N, nc.scalar.copy)
-        quantise(0, 1, 0, P, nc.scalar.copy)
-        quantise(0, 1, P, P, nc.scalar.copy)
+        gather_words(0, "root0")
+        quantise(0, 0, 0, N, nc.scalar.copy, "rs1")
+        gather_words(1, "rs1")
+        quantise(0, 1, 0, P, nc.scalar.copy, "square1", "word_window1")
+        quantise(0, 1, P, P, nc.scalar.copy, "raw00")
         mx = bank(6, [P, BLOCKS, P])
         sxx = bank(7, [P, BLOCKS, P])
-        wx = [wide("wx0"), wide("wx1")]
-        wxx = [wide("wxx0"), wide("wxx1")]
         wy = [wide("wy0"), wide("wy1")]
         wxy = [wide("wxy0"), wide("wxy1")]
         xsq, ys = wide("xsq"), wide("ys")
@@ -210,7 +209,9 @@ def tile_picked_ygwrg_coef_p_kernel(tc, x_words, x_scales, w1, w2, dist2, band, 
         ]
         xv = [[product(0, b, h, 2 * b + h) for h in range(HALVES)] for b in range(BLOCKS)]
         for g in range(PASSES):
-            quantise(1, g, 0, N, nc.scalar.copy)
+            quantise(1, g, 0, N, nc.scalar.copy, ("shared0", "root1")[g])
+        wx = [wide("wx0"), wide("wx1")]
+        wxx = [keep.tile([P, D, V], F32, name="wxx0", tag="root1", align_bytes=64), wide("wxx1")]
         yv1 = [product(1, 1, h, 4 + h) for h in range(HALVES)]
         for b in range(BLOCKS):
             for h in range(HALVES):
@@ -221,42 +222,51 @@ def tile_picked_ygwrg_coef_p_kernel(tc, x_words, x_scales, w1, w2, dist2, band, 
             nc.gpsimd.tensor_tensor(half(wxx[0], h), half(xsq, h), half(wt[0], h), ALU.mult)
         for h in range(HALVES):
             nc.vector.tensor_tensor(half(wxx[1], h), xv[1][h], half(wx[1], h), ALU.mult)
-        for h in range(1):
+        for h in range(2):
             nc.scalar.copy(half(ys, h), yv1[h])
             nc.gpsimd.tensor_tensor(half(wy[1], h), half(ys, h), half(wt[1], h), ALU.mult)
         nc.vector.tensor_tensor(km[:], mx[:], k1n[:], ALU.mult)
         nc.vector.tensor_tensor(dd[:], mx[:], km[:], ALU.mult)
         nc.scalar.activation(nn[:], mx[:], ACT.Identity, bias=1.0, scale=-0.2)
         for h in range(HALVES):
-            if h >= 1:
+            if h >= 2:
                 nc.vector.tensor_tensor(half(wy[1], h), yv1[h], half(wt[1], h), ALU.mult)
             nc.vector.tensor_tensor(half(wxy[1], h), yv1[h], half(wx[1], h), ALU.mult)
-        yv0 = [product(1, 0, h, (4, 5)[h]) for h in range(HALVES)]
+        yv0 = [product(1, 0, 0, (3, 5)[0])]
         for b in (1, 0):
             group_sum(sxx[:, b, :], wxx[b], [ridge[:, b, :]])
+        yv0.append(product(1, 0, 1, (3, 5)[1]))
         nc.vector.tensor_tensor(den[:], sxx[:], dd[:], ALU.add)
         nc.scalar.activation(ars[:], den[:], ACT.Abs_reciprocal_sqrt)
         nc.scalar.activation(rec[:], ars[:], ACT.Square)
         nc.vector.tensor_tensor(gg[:], nn[:], rec[:], ALU.mult)
         nc.vector.tensor_tensor(hk[:], gg[:], km[:], ALU.mult)
         my = bank(0, [P, BLOCKS, P])
-        sxy = [bank(2, [P, P]), bank(1, [P, P])]
+        sxy = [None, bank(1, [P, P])]
         group_sum(sxy[1][:], wxy[1])
         group_sum(my[:, 1, :], wy[1])
         for h in range(HALVES):
             nc.vector.tensor_tensor(half(wy[0], h), yv0[h], half(wt[0], h), ALU.mult)
+            nc.vector.tensor_tensor(half(wxy[0], h), yv0[h], half(wx[0], h), ALU.mult)
         group_sum(my[:, 0, :], wy[0])
-        nc.vector.tensor_tensor(half(wxy[0], 0), yv0[0], half(wx[0], 0), ALU.mult)
-        for dh in range(2):
-            ds = slice(4 * dh, 4 * dh + 4)
-            nc.vector.tensor_tensor(half(wxy[0], 1)[:, ds, :], yv0[1][:, ds, :], half(wx[0], 1)[:, ds, :], ALU.mult)
-        group_sum(sxy[0][:], wxy[0])
+        gg_turned = bank(2, [P, V])
+        nc.tensor.transpose(gg_turned[:], gg[:, 0], ident[:])
+        level = wxy[0]
+        for n in (4, 2, 1):
+            summed = keep.tile([P, n, V], F32, name="summed%d" % n)
+            nc.vector.tensor_tensor(summed[:], level[:, 0:n, :], level[:, n : 2 * n, :], ALU.add)
+            level = summed
         for b in (1, 0):
             nc.vector.scalar_tensor_tensor(t2[:, b], hk[:, b], 0.2, my[:, b], ALU.add, ALU.mult)
-            nc.vector.tensor_tensor(t1[:, b], sxy[b][:], gg[:, b], ALU.mult)
             turned = bank((6, 7)[b], [P, V])
-            nc.tensor.matmul(turned[:], t2[:, b], ident[:], start=True, stop=False, is_transpose=True)
-            nc.tensor.matmul(turned[:], t1[:, b], ident[:], start=False, stop=True, is_transpose=True)
             result = keep.tile([P, V], F32, name="result%d" % b)
-            nc.scalar.copy(result[:], turned[:])
+            if b == 1:
+                nc.vector.tensor_tensor(t1[:, b], sxy[b][:], gg[:, b], ALU.mult)
+                nc.tensor.matmul(turned[:], t2[:, b], ident[:], start=True, stop=False, is_transpose=True)
+                nc.tensor.matmul(turned[:], t1[:, b], ident[:], start=False, stop=True, is_transpose=True)
+                nc.scalar.copy(result[:], turned[:])
+            else:
+                nc.tensor.transpose(turned[:], t2[:, b], ident[:])
+                nc.vector.tensor_tensor(t1[:, b], gg_turned[:], level[:, 0, :], ALU.mult)
+                nc.vector.tensor_tensor(result[:], turned[:], t1[:, b], ALU.add)
             nc.sync.dma_start(out[P * b : P * (b + 1), :], result[:])

@@ -15,12 +15,17 @@ ACT = mybir.ActivationFunctionType
 
 K, T, S, D, N = 1024, 4096, 1024, 8, 256
 P = 128
-PASSES = 2
-BLOCKS = 2
-HALVES = 2
-HALF = 512
-V = 128
-VH = 64
+PACK = 4
+K_PASS = P * PACK
+PASSES = K // K_PASS
+SCALE_ROWS = 16
+QUADRANTS = 4
+BLOCKS = N // P
+CENTRES = S // D
+BANK = 512
+HALVES = S // BANK
+HALF_CENTRES = CENTRES // HALVES
+HALF_MEMBERS = D // 2
 FLOPS = 2 * 2 * K * N * S
 
 
@@ -30,243 +35,232 @@ def tile_picked_ygwrg_coef_p_kernel(tc, x_words, x_scales, w1, w2, dist2, band, 
         keep = ctx.enter_context(tc.tile_pool(name="keep", bufs=1))
         psum = ctx.enter_context(tc.psum_pool(name="psum", bufs=1))
 
+        def sbuf(name, shape, dtype, tag=None):
+            return keep.tile(shape, dtype, name=name, tag=tag or name, align_bytes=64)
+
         def bank(index, shape):
             return psum.tile(shape, F32, name="bank%d" % index, tag="bank%d" % index)
 
-        scale_window = keep.tile([P, T], U8, name="scale_window", tag="shared0", align_bytes=64)
+        def by_member(name, tag=None):
+            return sbuf(name, [P, D, CENTRES], F32, tag)
+
+        def by_centre(name, tag=None):
+            return sbuf(name, [P, BLOCKS, P], F32, tag)
+
+        def half(tile, h):
+            return tile[:, :, HALF_CENTRES * h : HALF_CENTRES * (h + 1)]
+
+        def add_transposed(dst, terms):
+            for i, term in enumerate(terms):
+                nc.tensor.matmul(dst, term, ident[:], start=(i == 0), stop=(i == len(terms) - 1), is_transpose=True)
+
+        def sum_members(dst, tile):
+            add_transposed(dst, [tile[:, d, :] for d in range(D)])
+
+        scale_rows = PASSES * SCALE_ROWS
+        scale_window = sbuf("scale_window", [P, T], U8)
         nc.sync.dma_start(
-            scale_window[0:32, :].bitcast(I32), x_scales.rearrange("g q c -> (g q) c").bitcast(I32)
+            scale_window[0:scale_rows, :].bitcast(I32), x_scales.rearrange("g q c -> (g q) c").bitcast(I32)
         )
-        dist_vd = keep.tile([P, D], F32, name="dist_vd")
-        nc.sync.dma_start(dist_vd[:], dist2[0].rearrange("(v d) -> v d", d=D))
+        dist = sbuf("dist", [P, D], F32)
+        nc.sync.dma_start(dist[:], dist2[0].rearrange("(v d) -> v d", d=D))
         offsets = keep.tile([P, S // 16], U16, name="offsets")
         nc.sync.dma_start(offsets[:], offs)
-        nc.gpsimd.memset(scale_window[32:64, :].bitcast(I32), 0)
-        nc.vector.memset(scale_window[64:P, :].bitcast(I32), 0)
-        band_pb = keep.tile([P, BLOCKS], F32, name="band_pb")
+        nc.gpsimd.memset(scale_window[scale_rows : P // 2, :].bitcast(I32), 0)
+        nc.vector.memset(scale_window[P // 2 : P, :].bitcast(I32), 0)
+        band_cols = sbuf("band_cols", [P, BLOCKS], F32)
         with nc.allow_non_contiguous_dma(reason="one value a partition"):
-            nc.scalar.dma_start(band_pb[:], band.rearrange("(b p) o -> p (b o)", p=P))
+            nc.scalar.dma_start(band_cols[:], band.rearrange("(b p) o -> p (b o)", p=P))
 
-        def load_words(g, tag):
-            t = keep.tile([P, T], I32, name="word_window%d" % g, tag=tag, align_bytes=64)
-            nc.sync.dma_start(t[:], x_words[g].rearrange("p c r -> p (c r)").bitcast(I32))
-            return t
+        def load_words(g):
+            window = sbuf("word_window%d" % g, [P, T], I32)
+            nc.sync.dma_start(window[:], x_words[g].rearrange("p c r -> p (c r)").bitcast(I32))
+            return window
 
-        def load_weights(mat, g, tag):
-            w = (w1, w2)[mat]
-            t = keep.tile([P, 4, N], F32, name="raw%d%d" % (mat, g), tag=tag, align_bytes=64)
-            nc.sync.dma_start(t[:], w[512 * g : 512 * (g + 1), :].rearrange("(p j) m -> p j m", j=4))
-            raw[mat, g] = t
+        def load_weights(name, w, g, tag=None):
+            raw = sbuf(name, [P, PACK, N], F32, tag)
+            nc.sync.dma_start(raw[:], w[K_PASS * g : K_PASS * (g + 1), :].rearrange("(p j) m -> p j m", j=PACK))
+            return raw
 
-        raw = {}
-        word_window = [load_words(0, "word_window0")]
-        load_weights(0, 0, "raw00")
-        word_window.append(load_words(1, "word_window1"))
+        word_window = [load_words(0)]
+        w1_raw = [load_weights("w1_raw0", w1, 0)]
+        word_window.append(load_words(1))
 
         ident = keep.tile([P, P], F32, name="ident")
         make_identity(nc, ident[:])
-        one = keep.tile([P, 1], F32, name="one")
-        nc.gpsimd.memset(one[:], 1.0)
-        table_preload = keep.tile([P, 1], F32, name="table_preload")
-        nc.scalar.activation(table_preload[:], one[:], ACT.Abs_reciprocal_sqrt)
+        five = keep.tile([P, 1], F32, name="five")
+        nc.gpsimd.memset(five[:], 5.0)
+        root_fifth = keep.tile([P, 1], F32, name="root_fifth")
+        nc.scalar.activation(root_fifth[:], five[:], ACT.Abs_reciprocal_sqrt)
 
-        picked_rows = keep.tile([P, S], U8, name="picked_rows", align_bytes=64)
+        picked_rows = sbuf("picked_rows", [P, S], U8)
         nc.vector.tensor_copy(picked_rows[:], scale_window[:].indirect(offsets[:]))
-        x_planes = []
+        x_scale = [sbuf("x_scale%d" % g, [P, S], U8) for g in range(PASSES)]
         for g in range(PASSES):
-            t = keep.tile([P, S], U8, name="x_planes%d" % g, align_bytes=64)
-            nc.gpsimd.memset(t[:].bitcast(I32), 0)
-            x_planes.append(t)
-        for g in range(PASSES):
-            for q in range(4):
-                first = 16 * g + 4 * q
-                (nc.sync, nc.gpsimd)[g].dma_start(
-                    x_planes[g][32 * q : 32 * q + 4, :].bitcast(I32),
-                    picked_rows[first : first + 4, :].bitcast(I32),
+            nc.gpsimd.memset(x_scale[g][:].bitcast(I32), 0)
+        for g, queue in enumerate((nc.sync, nc.gpsimd)):
+            for q in range(QUADRANTS):
+                first = SCALE_ROWS * g + 4 * q
+                queue.dma_start(
+                    x_scale[g][32 * q : 32 * q + 4, :].bitcast(I32), picked_rows[first : first + 4, :].bitcast(I32)
                 )
 
         dist_banks = []
         for dh in range(2):
-            t = bank(4 + dh, [P, 4, V])
-            for dl in range(4):
-                d = 4 * dh + dl
-                nc.tensor.transpose(t[:, dl, :], dist_vd[:, d : d + 1].to_broadcast([P, P]), ident[:])
-            dist_banks.append(t)
-        wt = []
-
-        def group_sum(dst, src, extra=()):
-            terms = [src[:, d, :] for d in range(D)] + list(extra)
-            for i, term in enumerate(terms):
-                nc.tensor.matmul(dst, term, ident[:], start=(i == 0), stop=(i == len(terms) - 1), is_transpose=True)
-
-        k1n = keep.tile([P, BLOCKS, P], F32, name="k1n")
-        ridge = keep.tile([P, BLOCKS, V], F32, name="ridge")
+            spread = bank(4 + dh, [P, HALF_MEMBERS, CENTRES])
+            for dl in range(HALF_MEMBERS):
+                d = HALF_MEMBERS * dh + dl
+                nc.tensor.transpose(spread[:, dl, :], dist[:, d : d + 1].to_broadcast([P, P]), ident[:])
+            dist_banks.append(spread)
+        members = [slice(HALF_MEMBERS * dh, HALF_MEMBERS * (dh + 1)) for dh in range(2)]
+        weight = []
+        sum_w = bank(6, [P, BLOCKS, P])
         for b in range(BLOCKS):
-            root = keep.tile([P, D, V], F32, name="root%d" % b, tag="root%d" % b, align_bytes=64)
-            square = keep.tile([P, D, V], F32, name="square%d" % b, tag="square%d" % b, align_bytes=64)
+            root = by_member("root%d" % b)
+            weight.append(by_member("weight%d" % b))
             for dh in range(2):
                 nc.scalar.activation(
-                    root[:, 4 * dh : 4 * dh + 4, :], dist_banks[dh][:], ACT.Relu, bias=1.3, scale=band_pb[:, b : b + 1]
+                    root[:, members[dh], :], dist_banks[dh][:], ACT.Relu, bias=1.3, scale=band_cols[:, b : b + 1]
                 )
-            for dh in range(2):
-                ds = slice(4 * dh, 4 * dh + 4)
+            for ds in members:
                 if b == 0:
-                    nc.vector.tensor_tensor(square[:, ds, :], root[:, ds, :], root[:, ds, :], ALU.mult)
+                    nc.vector.tensor_tensor(weight[b][:, ds, :], root[:, ds, :], root[:, ds, :], ALU.mult)
                 else:
-                    nc.scalar.activation(square[:, ds, :], root[:, ds, :], ACT.Square)
-            s0_bank = bank((2, 6)[b], [P, P])
-            group_sum(s0_bank[:], square)
-            q = keep.tile([P, P], F32, name="q%d" % b, tag="q%d" % b, align_bytes=64)
-            rs = keep.tile([P, P], F32, name="rs%d" % b, tag="rs%d" % b, align_bytes=64)
-            nc.scalar.activation(q[:], s0_bank[:], ACT.Abs_reciprocal_sqrt, bias=0.2)
-            nc.scalar.activation(rs[:], q[:], ACT.Square)
-            rs_bank = bank((3, 7)[b], [P, V])
-            nc.tensor.transpose(rs_bank[:], rs[:], ident[:])
-            t = keep.tile([P, D, V], F32, name="wt%d" % b)
-            nc.vector.tensor_tensor(
-                t[:], square[:], rs_bank[:].unsqueeze(1).to_broadcast([P, D, V]), ALU.mult
-            )
-            nc.scalar.activation(k1n[:, b, :], rs[:], ACT.Identity, scale=-0.2, bias=-1.0)
-            nc.scalar.activation(ridge[:, b, :], rs_bank[:], ACT.Copy, scale=0.3)
-            wt.append(t)
-        load_weights(0, 1, "shared0")
-        load_weights(1, 0, "root1")
-        load_weights(1, 1, "q0")
+                    nc.scalar.activation(weight[b][:, ds, :], root[:, ds, :], ACT.Square)
+            sum_members(sum_w[:, b, :], weight[b])
 
-        words = {}
+        w1_raw.append(load_weights("w1_raw1", w1, 1, tag="scale_window"))
+        w2_raw = [load_weights("w2_raw0", w2, 0, tag="dist"), load_weights("w2_raw1", w2, 1, tag="band_cols")]
+
+        rsqrt_s0, inv_s0, shrink, shrink_plus_1, centre = [
+            by_centre(name) for name in ("rsqrt_s0", "inv_s0", "shrink", "shrink_plus_1", "centre")
+        ]
+        nc.scalar.activation(rsqrt_s0[:], sum_w[:], ACT.Abs_reciprocal_sqrt, bias=0.2)
+        nc.scalar.activation(inv_s0[:], rsqrt_s0[:], ACT.Square)
+        nc.scalar.activation(shrink[:], rsqrt_s0[:], ACT.Square, scale=root_fifth[:])
+        nc.scalar.activation(shrink_plus_1[:], shrink[:], ACT.Identity, bias=1.0)
+        nc.gpsimd.tensor_tensor(centre[:], shrink_plus_1[:], inv_s0[:], ALU.mult)
 
         def gather_words(g, tag):
-            t = keep.tile([P, S], U32, name="words%d" % g, tag=tag, align_bytes=64)
-            nc.vector.tensor_copy(t[:], word_window[g][:].bitcast(U32).indirect(offsets[:]))
-            for h in range(HALVES):
-                words[g, h] = t[:, HALF * h : HALF * (h + 1)]
+            picked = sbuf("x_codes%d" % g, [P, S], U32, tag)
+            nc.vector.tensor_copy(picked[:], word_window[g][:].bitcast(U32).indirect(offsets[:]))
+            return picked
 
-        codes, planes = {}, {}
-
-        def quantise(mat, g, first, width, cast, tag=None, code_tag=None):
-            name = "%d%d%d" % (mat, g, first)
-            grouped = keep.tile([P, width, 4], BF16, name="grouped" + name, tag=tag or "grouped" + name, align_bytes=64)
-            cast(
-                grouped[:].rearrange("p (c i) j -> p c j i", i=4),
-                raw[mat, g][:, :, first : first + width].rearrange("p j (c i) -> p c j i", i=4),
+        def quantise(name, raw, grouped):
+            width = raw.shape[2]
+            nc.scalar.copy(
+                grouped.rearrange("p (c i) j -> p c j i", i=4), raw.rearrange("p j (c i) -> p c j i", i=4)
             )
-            c = keep.tile([P, width], U32, name="codes" + name, tag=code_tag or "codes" + name, align_bytes=64)
-            s = keep.tile([P, width], U8, name="planes" + name, align_bytes=64)
-            nc.vector.quantize_mx(c[:].bitcast(FP8X4), s[:], grouped[:].rearrange("p m j -> p (m j)"))
-            for m0 in range(0, width, P):
-                codes[mat, g, (first + m0) // P] = c[:, m0 : m0 + P]
-                planes[mat, g, (first + m0) // P] = s[:, m0 : m0 + P]
+            codes = sbuf(name + "_codes", [P, width], U32)
+            scales = sbuf(name + "_scales", [P, width], U8)
+            nc.vector.quantize_mx(codes[:].bitcast(FP8X4), scales[:], grouped.rearrange("p m j -> p (m j)"))
+            return [(codes[:, m : m + P], scales[:, m : m + P]) for m in range(0, width, P)]
 
-        def product(mat, b, h, index):
-            t = bank(index, [P, HALF])
+        def product(operands, b, h, index):
+            acc = bank(index, [P, BANK])
+            cols = slice(BANK * h, BANK * (h + 1))
             for g in range(PASSES):
+                codes, scales = operands[g][b]
                 nc.tensor.matmul_mx(
-                    t[:],
-                    lhsT=codes[mat, g, b].bitcast(FP8X4),
-                    lhsT_scale=planes[mat, g, b],
-                    rhs=words[g, h].bitcast(FP8X4),
-                    rhs_scale=x_planes[g][:, HALF * h : HALF * (h + 1)],
+                    acc[:],
+                    lhsT=codes.bitcast(FP8X4),
+                    lhsT_scale=scales,
+                    rhs=x_codes[g][:, cols].bitcast(FP8X4),
+                    rhs_scale=x_scale[g][:, cols],
                     start=(g == 0),
                     stop=(g == PASSES - 1),
                 )
-            return t[:].rearrange("p (v d) -> p d v", d=D)
+            return acc[:].rearrange("p (v d) -> p d v", d=D)
 
-        def half(t, h):
-            return t[:, :, VH * h : VH * (h + 1)]
+        x_codes = [gather_words(0, tag="root0")]
+        w1_first = sbuf("w1_first", [P, N, PACK], BF16, tag="root1")
+        w1_mx = [quantise("w1_0", w1_raw[0][:], w1_first[:])]
+        x_codes.append(gather_words(1, tag="root1"))
+        casts = sbuf("casts", [P, 2 * N, PACK], BF16, tag="rsqrt_s0")
+        w1_mx.append([])
+        for b in range(BLOCKS):
+            models = slice(P * b, P * (b + 1))
+            w1_mx[1].extend(quantise("w1_1%d" % b, w1_raw[1][:, :, models], casts[:, models, :]))
 
-
-        def wide(name):
-            return keep.tile([P, D, V], F32, name=name)
-
-        def small(name):
-            return keep.tile([P, BLOCKS, P], F32, name=name)
-
-        def warm_up(index):
-            t = bank(index, [P, HALF])
-            for g in range(PASSES):
-                nc.tensor.matmul_mx(
-                    t[:],
-                    lhsT=words[1, 0][:, 0:P].bitcast(FP8X4),
-                    lhsT_scale=x_planes[1][:, 0:P],
-                    rhs=words[g, 0][:].bitcast(FP8X4),
-                    rhs_scale=x_planes[g][:, 0:HALF],
-                    start=(g == 0),
-                    stop=(g == PASSES - 1),
-                )
-
-        gather_words(0, "root0")
-        quantise(0, 0, 0, N, nc.scalar.copy, "rs1")
-        gather_words(1, "rs1")
-        quantise(0, 1, 0, P, nc.scalar.copy, "square1", "word_window1")
-        quantise(0, 1, P, P, nc.scalar.copy, "raw00")
-        mx = bank(6, [P, BLOCKS, P])
-        sxx = bank(7, [P, BLOCKS, P])
-        wy = [wide("wy0"), wide("wy1")]
-        wxy = [wide("wxy0"), wide("wxy1")]
-        xsq, ys = wide("xsq"), wide("ys")
-        km, dd, nn, den, ars, rec, gg, hk, t1, t2 = [
-            small(n) for n in ("km", "dd", "nn", "den", "ars", "rec", "gg", "hk", "t1", "t2")
-        ]
-        xv = [[product(0, b, h, 2 * b + h) for h in range(HALVES)] for b in range(BLOCKS)]
-        for g in range(PASSES):
-            quantise(1, g, 0, N, nc.scalar.copy, ("shared0", "root1")[g])
-        wx = [wide("wx0"), wide("wx1")]
-        wxx = [keep.tile([P, D, V], F32, name="wxx0", tag="root1", align_bytes=64), wide("wxx1")]
-        yv1 = [product(1, 1, h, 4 + h) for h in range(HALVES)]
+        sum_x = bank(6, [P, BLOCKS, P])
+        sum_xx = bank(7, [P, BLOCKS, P])
+        x = [[product(w1_mx, b, h, HALVES * b + h) for h in range(HALVES)] for b in range(BLOCKS)]
+        w2_mx = [quantise("w2_0", w2_raw[0][:], casts[:, N : 2 * N, :])]
+        w2_last = sbuf("w2_last", [P, N, PACK], BF16, tag="dist")
+        w2_mx.append(quantise("w2_1", w2_raw[1][:], w2_last[:]))
+        wx = [by_member("wx0"), by_member("wx1", tag="rsqrt_s0")]
+        x_squared = by_member("x_squared", tag="band_cols")
+        wxx_both = sbuf("wxx", [P, BLOCKS * D, CENTRES], F32, tag="dist")
+        wxx = [wxx_both[:, D * b : D * (b + 1), :] for b in range(BLOCKS)]
+        y1 = [product(w2_mx, 1, h, 4 + h) for h in range(HALVES)]
         for b in range(BLOCKS):
             for h in range(HALVES):
-                nc.vector.tensor_tensor(half(wx[b], h), xv[b][h], half(wt[b], h), ALU.mult)
-            group_sum(mx[:, b, :], wx[b])
+                nc.vector.tensor_tensor(half(wx[b], h), x[b][h], half(weight[b], h), ALU.mult)
+            sum_members(sum_x[:, b, :], wx[b])
+
+        wy = [by_member("wy0"), by_member("wy1")]
+        wxy = [by_member("wxy0"), by_member("wxy1")]
+        y1_copy = by_member("y1_copy")
         for h in range(HALVES):
-            nc.scalar.activation(half(xsq, h), xv[0][h], ACT.Square)
-            nc.gpsimd.tensor_tensor(half(wxx[0], h), half(xsq, h), half(wt[0], h), ALU.mult)
+            nc.scalar.activation(half(x_squared, h), x[0][h], ACT.Square)
+            nc.gpsimd.tensor_tensor(half(wxx[0], h), half(x_squared, h), half(weight[0], h), ALU.mult)
         for h in range(HALVES):
-            nc.vector.tensor_tensor(half(wxx[1], h), xv[1][h], half(wx[1], h), ALU.mult)
-        for h in range(2):
-            nc.scalar.copy(half(ys, h), yv1[h])
-            nc.gpsimd.tensor_tensor(half(wy[1], h), half(ys, h), half(wt[1], h), ALU.mult)
-        nc.vector.tensor_tensor(km[:], mx[:], k1n[:], ALU.mult)
-        nc.vector.tensor_tensor(dd[:], mx[:], km[:], ALU.mult)
-        nc.scalar.activation(nn[:], mx[:], ACT.Identity, bias=1.0, scale=-0.2)
+            nc.vector.tensor_tensor(half(wxx[1], h), x[1][h], half(wx[1], h), ALU.mult)
         for h in range(HALVES):
-            if h >= 2:
-                nc.vector.tensor_tensor(half(wy[1], h), yv1[h], half(wt[1], h), ALU.mult)
-            nc.vector.tensor_tensor(half(wxy[1], h), yv1[h], half(wx[1], h), ALU.mult)
-        yv0 = [product(1, 0, 0, (3, 5)[0])]
+            nc.scalar.copy(half(y1_copy, h), y1[h])
+            nc.gpsimd.tensor_tensor(half(wy[1], h), half(y1_copy, h), half(weight[1], h), ALU.mult)
+
+        centre_x, shrink_x, centre_xx, top, sxx, rsqrt_bottom, inv_bottom, gain, gain_centre_x = [
+            by_centre(name)
+            for name in (
+                "centre_x", "shrink_x", "centre_xx", "top", "sxx", "rsqrt_bottom", "inv_bottom", "gain", "gain_centre_x"
+            )
+        ]
+        nc.vector.tensor_tensor(centre_x[:], sum_x[:], centre[:], ALU.mult)
+        nc.vector.tensor_tensor(shrink_x[:], sum_x[:], shrink[:], ALU.mult)
+        nc.vector.tensor_tensor(centre_xx[:], sum_x[:], centre_x[:], ALU.mult)
+        nc.scalar.activation(top[:], shrink_x[:], ACT.Identity, bias=1.0, scale=-1.0)
+        for h in range(HALVES):
+            nc.vector.tensor_tensor(half(wxy[1], h), y1[h], half(wx[1], h), ALU.mult)
+
+        y0 = [product(w2_mx, 0, 0, 3)]
         for b in (1, 0):
-            group_sum(sxx[:, b, :], wxx[b], [ridge[:, b, :]])
-        yv0.append(product(1, 0, 1, (3, 5)[1]))
-        nc.vector.tensor_tensor(den[:], sxx[:], dd[:], ALU.add)
-        nc.scalar.activation(ars[:], den[:], ACT.Abs_reciprocal_sqrt)
-        nc.scalar.activation(rec[:], ars[:], ACT.Square)
-        nc.vector.tensor_tensor(gg[:], nn[:], rec[:], ALU.mult)
-        nc.vector.tensor_tensor(hk[:], gg[:], km[:], ALU.mult)
-        my = bank(0, [P, BLOCKS, P])
-        sxy = [None, bank(1, [P, P])]
-        group_sum(sxy[1][:], wxy[1])
-        group_sum(my[:, 1, :], wy[1])
+            sum_members(sum_xx[:, b, :], wxx[b])
+        y0.append(product(w2_mx, 0, 1, 5))
+        nc.vector.tensor_tensor(sxx[:], sum_xx[:], centre_xx[:], ALU.subtract)
+        nc.scalar.activation(rsqrt_bottom[:], sxx[:], ACT.Abs_reciprocal_sqrt, bias=0.3)
+        nc.scalar.activation(inv_bottom[:], rsqrt_bottom[:], ACT.Square)
+        nc.vector.tensor_tensor(gain[:], top[:], inv_bottom[:], ALU.mult)
+        nc.vector.tensor_tensor(gain_centre_x[:], gain[:], centre_x[:], ALU.mult)
+
+        sum_y = bank(0, [P, BLOCKS, P])
+        sum_xy1 = bank(1, [P, P])
+        sum_members(sum_y[:, 1, :], wy[1])
         for h in range(HALVES):
-            nc.vector.tensor_tensor(half(wy[0], h), yv0[h], half(wt[0], h), ALU.mult)
-            nc.vector.tensor_tensor(half(wxy[0], h), yv0[h], half(wx[0], h), ALU.mult)
-        group_sum(my[:, 0, :], wy[0])
-        gg_turned = bank(2, [P, V])
-        nc.tensor.transpose(gg_turned[:], gg[:, 0], ident[:])
-        level = wxy[0]
-        for n in (4, 2, 1):
-            summed = keep.tile([P, n, V], F32, name="summed%d" % n)
-            nc.vector.tensor_tensor(summed[:], level[:, 0:n, :], level[:, n : 2 * n, :], ALU.add)
-            level = summed
-        for b in (1, 0):
-            nc.vector.scalar_tensor_tensor(t2[:, b], hk[:, b], 0.2, my[:, b], ALU.add, ALU.mult)
-            turned = bank((6, 7)[b], [P, V])
-            result = keep.tile([P, V], F32, name="result%d" % b)
-            if b == 1:
-                nc.vector.tensor_tensor(t1[:, b], sxy[b][:], gg[:, b], ALU.mult)
-                nc.tensor.matmul(turned[:], t2[:, b], ident[:], start=True, stop=False, is_transpose=True)
-                nc.tensor.matmul(turned[:], t1[:, b], ident[:], start=False, stop=True, is_transpose=True)
-                nc.scalar.copy(result[:], turned[:])
-            else:
-                nc.tensor.transpose(turned[:], t2[:, b], ident[:])
-                nc.vector.tensor_tensor(t1[:, b], gg_turned[:], level[:, 0, :], ALU.mult)
-                nc.vector.tensor_tensor(result[:], turned[:], t1[:, b], ALU.add)
-            nc.sync.dma_start(out[P * b : P * (b + 1), :], result[:])
+            nc.vector.tensor_tensor(half(wy[0], h), y0[h], half(weight[0], h), ALU.mult)
+            nc.vector.tensor_tensor(half(wxy[0], h), y0[h], half(wx[0], h), ALU.mult)
+        sum_members(sum_y[:, 0, :], wy[0])
+        sum_members(sum_xy1[:], wxy[1])
+        gain0_turned = bank(2, [P, CENTRES])
+        nc.tensor.transpose(gain0_turned[:], gain[:, 0], ident[:])
+
+        shrink_y, cross_y = by_centre("shrink_y"), by_centre("cross_y")
+        gain_xy0, gain_xy1 = sbuf("gain_xy0", [P, CENTRES], F32), sbuf("gain_xy1", [P, P], F32)
+        nc.vector.tensor_tensor(shrink_y[:], sum_y[:], shrink[:], ALU.mult)
+        nc.vector.scalar_tensor_tensor(cross_y[:], gain_centre_x[:], -1.0, sum_y[:], ALU.mult, ALU.mult)
+        nc.vector.tensor_tensor(gain_xy1[:], sum_xy1[:], gain[:, 1], ALU.mult)
+        turned = [bank(6 + b, [P, CENTRES]) for b in range(BLOCKS)]
+        result = [sbuf("result%d" % b, [P, CENTRES], F32) for b in range(BLOCKS)]
+        add_transposed(turned[0][:], [shrink_y[:, 0], cross_y[:, 0]])
+        add_transposed(turned[1][:], [shrink_y[:, 1], cross_y[:, 1], gain_xy1[:]])
+        nc.scalar.copy(result[1][:], turned[1][:])
+        nc.sync.dma_start(out[P : 2 * P, :], result[1][:])
+
+        partial = wxy[0]
+        for n in (D // 2, D // 4, D // 8):
+            folded = sbuf("folded%d" % n, [P, n, CENTRES], F32)
+            nc.vector.tensor_tensor(folded[:], partial[:, 0:n, :], partial[:, n : 2 * n, :], ALU.add)
+            partial = folded
+        nc.vector.tensor_tensor(gain_xy0[:], gain0_turned[:], partial[:, 0, :], ALU.mult)
+        nc.vector.tensor_tensor(result[0][:], turned[0][:], gain_xy0[:], ALU.add)
+        nc.sync.dma_start(out[0:P, :], result[0][:])

from contextlib import ExitStack

import concourse.mybir as mybir
from concourse.masks import make_identity

F32 = mybir.dt.float32
BF16 = mybir.dt.bfloat16
I32 = mybir.dt.int32
U32 = mybir.dt.uint32
U16 = mybir.dt.uint16
U8 = mybir.dt.uint8
FP8X4 = mybir.dt.float8_e4m3fn_x4
ALU = mybir.AluOpType
ACT = mybir.ActivationFunctionType

K, T, S, D, N = 1024, 4096, 1024, 8, 256
P = 128
PACK = 4
K_PASS = P * PACK
PASSES = K // K_PASS
SCALE_ROWS = 16
QUADRANTS = 4
BLOCKS = N // P
CENTRES = S // D
BANK = 512
HALVES = S // BANK
HALF_CENTRES = CENTRES // HALVES
HALF_MEMBERS = D // 2
FLOPS = 2 * 2 * K * N * S


def tile_picked_ygwrg_coef_p_kernel(tc, x_words, x_scales, w1, w2, dist2, band, offs, out):
    nc = tc.nc
    with ExitStack() as ctx:
        keep = ctx.enter_context(tc.tile_pool(name="keep", bufs=1))
        psum = ctx.enter_context(tc.psum_pool(name="psum", bufs=1))

        def sbuf(name, shape, dtype, tag=None):
            return keep.tile(shape, dtype, name=name, tag=tag or name, align_bytes=64)

        def bank(index, shape):
            return psum.tile(shape, F32, name="bank%d" % index, tag="bank%d" % index)

        def by_member(name, tag=None):
            return sbuf(name, [P, D, CENTRES], F32, tag)

        def by_centre(name, tag=None):
            return sbuf(name, [P, BLOCKS, P], F32, tag)

        def half(tile, h):
            return tile[:, :, HALF_CENTRES * h : HALF_CENTRES * (h + 1)]

        def add_transposed(dst, terms):
            for i, term in enumerate(terms):
                nc.tensor.matmul(dst, term, ident[:], start=(i == 0), stop=(i == len(terms) - 1), is_transpose=True)

        def sum_members(dst, tile):
            add_transposed(dst, [tile[:, d, :] for d in range(D)])

        scale_rows = PASSES * SCALE_ROWS
        scale_window = sbuf("scale_window", [P, T], U8)
        nc.sync.dma_start(
            scale_window[0:scale_rows, :].bitcast(I32), x_scales.rearrange("g q c -> (g q) c").bitcast(I32)
        )
        dist = sbuf("dist", [P, D], F32)
        nc.sync.dma_start(dist[:], dist2[0].rearrange("(v d) -> v d", d=D))
        offsets = keep.tile([P, S // 16], U16, name="offsets")
        nc.sync.dma_start(offsets[:], offs)
        nc.gpsimd.memset(scale_window[scale_rows : P // 2, :].bitcast(I32), 0)
        nc.vector.memset(scale_window[P // 2 : P, :].bitcast(I32), 0)
        band_cols = sbuf("band_cols", [P, BLOCKS], F32)
        with nc.allow_non_contiguous_dma(reason="one value a partition"):
            nc.scalar.dma_start(band_cols[:], band.rearrange("(b p) o -> p (b o)", p=P))

        def load_words(g):
            window = sbuf("word_window%d" % g, [P, T], I32)
            nc.sync.dma_start(window[:], x_words[g].rearrange("p c r -> p (c r)").bitcast(I32))
            return window

        def load_weights(name, w, g, tag=None):
            raw = sbuf(name, [P, PACK, N], F32, tag)
            nc.sync.dma_start(raw[:], w[K_PASS * g : K_PASS * (g + 1), :].rearrange("(p j) m -> p j m", j=PACK))
            return raw

        word_window = [load_words(0)]
        w1_raw = [load_weights("w1_raw0", w1, 0)]
        word_window.append(load_words(1))

        ident = keep.tile([P, P], F32, name="ident")
        make_identity(nc, ident[:])
        five = keep.tile([P, 1], F32, name="five")
        nc.gpsimd.memset(five[:], 5.0)
        root_fifth = keep.tile([P, 1], F32, name="root_fifth")
        nc.scalar.activation(root_fifth[:], five[:], ACT.Abs_reciprocal_sqrt)

        picked_rows = sbuf("picked_rows", [P, S], U8)
        nc.vector.tensor_copy(picked_rows[:], scale_window[:].indirect(offsets[:]))
        x_scale = [sbuf("x_scale%d" % g, [P, S], U8) for g in range(PASSES)]
        for g in range(PASSES):
            nc.gpsimd.memset(x_scale[g][:].bitcast(I32), 0)
        for g, queue in enumerate((nc.sync, nc.gpsimd)):
            for q in range(QUADRANTS):
                first = SCALE_ROWS * g + 4 * q
                queue.dma_start(
                    x_scale[g][32 * q : 32 * q + 4, :].bitcast(I32), picked_rows[first : first + 4, :].bitcast(I32)
                )

        dist_banks = []
        for dh in range(2):
            spread = bank(4 + dh, [P, HALF_MEMBERS, CENTRES])
            for dl in range(HALF_MEMBERS):
                d = HALF_MEMBERS * dh + dl
                nc.tensor.transpose(spread[:, dl, :], dist[:, d : d + 1].to_broadcast([P, P]), ident[:])
            dist_banks.append(spread)
        members = [slice(HALF_MEMBERS * dh, HALF_MEMBERS * (dh + 1)) for dh in range(2)]
        weight = []
        sum_w = bank(6, [P, BLOCKS, P])
        for b in range(BLOCKS):
            root = by_member("root%d" % b)
            weight.append(by_member("weight%d" % b))
            for dh in range(2):
                nc.scalar.activation(
                    root[:, members[dh], :], dist_banks[dh][:], ACT.Relu, bias=1.3, scale=band_cols[:, b : b + 1]
                )
            for ds in members:
                if b == 0:
                    nc.vector.tensor_tensor(weight[b][:, ds, :], root[:, ds, :], root[:, ds, :], ALU.mult)
                else:
                    nc.scalar.activation(weight[b][:, ds, :], root[:, ds, :], ACT.Square)
            sum_members(sum_w[:, b, :], weight[b])

        w1_raw.append(load_weights("w1_raw1", w1, 1, tag="scale_window"))
        w2_raw = [load_weights("w2_raw0", w2, 0, tag="dist"), load_weights("w2_raw1", w2, 1, tag="band_cols")]

        rsqrt_s0, inv_s0, shrink, shrink_plus_1, centre = [
            by_centre(name) for name in ("rsqrt_s0", "inv_s0", "shrink", "shrink_plus_1", "centre")
        ]
        nc.scalar.activation(rsqrt_s0[:], sum_w[:], ACT.Abs_reciprocal_sqrt, bias=0.2)
        nc.scalar.activation(inv_s0[:], rsqrt_s0[:], ACT.Square)
        nc.scalar.activation(shrink[:], rsqrt_s0[:], ACT.Square, scale=root_fifth[:])
        nc.scalar.activation(shrink_plus_1[:], shrink[:], ACT.Identity, bias=1.0)
        nc.gpsimd.tensor_tensor(centre[:], shrink_plus_1[:], inv_s0[:], ALU.mult)

        def gather_words(g, tag):
            picked = sbuf("x_codes%d" % g, [P, S], U32, tag)
            nc.vector.tensor_copy(picked[:], word_window[g][:].bitcast(U32).indirect(offsets[:]))
            return picked

        def quantise(name, raw, grouped):
            width = raw.shape[2]
            nc.scalar.copy(
                grouped.rearrange("p (c i) j -> p c j i", i=4), raw.rearrange("p j (c i) -> p c j i", i=4)
            )
            codes = sbuf(name + "_codes", [P, width], U32)
            scales = sbuf(name + "_scales", [P, width], U8)
            nc.vector.quantize_mx(codes[:].bitcast(FP8X4), scales[:], grouped.rearrange("p m j -> p (m j)"))
            return [(codes[:, m : m + P], scales[:, m : m + P]) for m in range(0, width, P)]

        def product(operands, b, h, index):
            acc = bank(index, [P, BANK])
            cols = slice(BANK * h, BANK * (h + 1))
            for g in range(PASSES):
                codes, scales = operands[g][b]
                nc.tensor.matmul_mx(
                    acc[:],
                    lhsT=codes.bitcast(FP8X4),
                    lhsT_scale=scales,
                    rhs=x_codes[g][:, cols].bitcast(FP8X4),
                    rhs_scale=x_scale[g][:, cols],
                    start=(g == 0),
                    stop=(g == PASSES - 1),
                )
            return acc[:].rearrange("p (v d) -> p d v", d=D)

        x_codes = [gather_words(0, tag="root0")]
        w1_first = sbuf("w1_first", [P, N, PACK], BF16, tag="root1")
        w1_mx = [quantise("w1_0", w1_raw[0][:], w1_first[:])]
        x_codes.append(gather_words(1, tag="root1"))
        casts = sbuf("casts", [P, 2 * N, PACK], BF16, tag="rsqrt_s0")
        w1_mx.append([])
        for b in range(BLOCKS):
            models = slice(P * b, P * (b + 1))
            w1_mx[1].extend(quantise("w1_1%d" % b, w1_raw[1][:, :, models], casts[:, models, :]))

        sum_x = bank(6, [P, BLOCKS, P])
        sum_xx = bank(7, [P, BLOCKS, P])
        x = [[product(w1_mx, b, h, HALVES * b + h) for h in range(HALVES)] for b in range(BLOCKS)]
        w2_mx = [quantise("w2_0", w2_raw[0][:], casts[:, N : 2 * N, :])]
        w2_last = sbuf("w2_last", [P, N, PACK], BF16, tag="dist")
        w2_mx.append(quantise("w2_1", w2_raw[1][:], w2_last[:]))
        wx = [by_member("wx0"), by_member("wx1", tag="rsqrt_s0")]
        x_squared = by_member("x_squared", tag="band_cols")
        wxx_both = sbuf("wxx", [P, BLOCKS * D, CENTRES], F32, tag="dist")
        wxx = [wxx_both[:, D * b : D * (b + 1), :] for b in range(BLOCKS)]
        y1 = [product(w2_mx, 1, h, 4 + h) for h in range(HALVES)]
        for b in range(BLOCKS):
            for h in range(HALVES):
                nc.vector.tensor_tensor(half(wx[b], h), x[b][h], half(weight[b], h), ALU.mult)
            sum_members(sum_x[:, b, :], wx[b])

        wy = [by_member("wy0"), by_member("wy1")]
        wxy = [by_member("wxy0"), by_member("wxy1")]
        y1_copy = by_member("y1_copy")
        for h in range(HALVES):
            nc.scalar.activation(half(x_squared, h), x[0][h], ACT.Square)
            nc.gpsimd.tensor_tensor(half(wxx[0], h), half(x_squared, h), half(weight[0], h), ALU.mult)
        for h in range(HALVES):
            nc.vector.tensor_tensor(half(wxx[1], h), x[1][h], half(wx[1], h), ALU.mult)
        for h in range(HALVES):
            nc.scalar.copy(half(y1_copy, h), y1[h])
            nc.gpsimd.tensor_tensor(half(wy[1], h), half(y1_copy, h), half(weight[1], h), ALU.mult)

        centre_x, shrink_x, centre_xx, top, sxx, rsqrt_bottom, inv_bottom, gain, gain_centre_x = [
            by_centre(name)
            for name in (
                "centre_x", "shrink_x", "centre_xx", "top", "sxx", "rsqrt_bottom", "inv_bottom", "gain", "gain_centre_x"
            )
        ]
        nc.vector.tensor_tensor(centre_x[:], sum_x[:], centre[:], ALU.mult)
        nc.vector.tensor_tensor(shrink_x[:], sum_x[:], shrink[:], ALU.mult)
        nc.vector.tensor_tensor(centre_xx[:], sum_x[:], centre_x[:], ALU.mult)
        nc.scalar.activation(top[:], shrink_x[:], ACT.Identity, bias=1.0, scale=-1.0)
        for h in range(HALVES):
            nc.vector.tensor_tensor(half(wxy[1], h), y1[h], half(wx[1], h), ALU.mult)

        y0 = [product(w2_mx, 0, 0, 3)]
        for b in (1, 0):
            sum_members(sum_xx[:, b, :], wxx[b])
        y0.append(product(w2_mx, 0, 1, 5))
        nc.vector.tensor_tensor(sxx[:], sum_xx[:], centre_xx[:], ALU.subtract)
        nc.scalar.activation(rsqrt_bottom[:], sxx[:], ACT.Abs_reciprocal_sqrt, bias=0.3)
        nc.scalar.activation(inv_bottom[:], rsqrt_bottom[:], ACT.Square)
        nc.vector.tensor_tensor(gain[:], top[:], inv_bottom[:], ALU.mult)
        nc.vector.tensor_tensor(gain_centre_x[:], gain[:], centre_x[:], ALU.mult)

        sum_y = bank(0, [P, BLOCKS, P])
        sum_xy1 = bank(1, [P, P])
        sum_members(sum_y[:, 1, :], wy[1])
        for h in range(HALVES):
            nc.vector.tensor_tensor(half(wy[0], h), y0[h], half(weight[0], h), ALU.mult)
            nc.vector.tensor_tensor(half(wxy[0], h), y0[h], half(wx[0], h), ALU.mult)
        sum_members(sum_y[:, 0, :], wy[0])
        sum_members(sum_xy1[:], wxy[1])
        gain0_turned = bank(2, [P, CENTRES])
        nc.tensor.transpose(gain0_turned[:], gain[:, 0], ident[:])

        shrink_y, cross_y = by_centre("shrink_y"), by_centre("cross_y")
        gain_xy0, gain_xy1 = sbuf("gain_xy0", [P, CENTRES], F32), sbuf("gain_xy1", [P, P], F32)
        nc.vector.tensor_tensor(shrink_y[:], sum_y[:], shrink[:], ALU.mult)
        nc.vector.scalar_tensor_tensor(cross_y[:], gain_centre_x[:], -1.0, sum_y[:], ALU.mult, ALU.mult)
        nc.vector.tensor_tensor(gain_xy1[:], sum_xy1[:], gain[:, 1], ALU.mult)
        turned = [bank(6 + b, [P, CENTRES]) for b in range(BLOCKS)]
        result = [sbuf("result%d" % b, [P, CENTRES], F32) for b in range(BLOCKS)]
        add_transposed(turned[0][:], [shrink_y[:, 0], cross_y[:, 0]])
        add_transposed(turned[1][:], [shrink_y[:, 1], cross_y[:, 1], gain_xy1[:]])
        nc.scalar.copy(result[1][:], turned[1][:])
        nc.sync.dma_start(out[P : 2 * P, :], result[1][:])

        partial = wxy[0]
        for n in (D // 2, D // 4, D // 8):
            folded = sbuf("folded%d" % n, [P, n, CENTRES], F32)
            nc.vector.tensor_tensor(folded[:], partial[:, 0:n, :], partial[:, n : 2 * n, :], ALU.add)
            partial = folded
        nc.vector.tensor_tensor(gain_xy0[:], gain0_turned[:], partial[:, 0, :], ALU.mult)
        nc.vector.tensor_tensor(result[0][:], turned[0][:], gain_xy0[:], ALU.add)
        nc.sync.dma_start(out[0:P, :], result[0][:])
